import numpy as np
import ml_dtypes


def mxq(x, axis, fmt="e4m3"):
    dtype, down = {"e4m3": (ml_dtypes.float8_e4m3fn, 7), "e5m2": (ml_dtypes.float8_e5m2, 14)}[fmt]
    v = np.moveaxis(np.asarray(x, np.float32).astype(ml_dtypes.bfloat16).astype(np.float64), axis, -1)
    blocks = v.reshape(v.shape[:-1] + (-1, 32))
    amax = np.abs(blocks).max(-1, keepdims=True)
    byte = np.maximum(np.where(amax > 0, np.frexp(amax)[1] - 1 + 127, 0) - down, 1)
    scale = np.exp2(byte - 127.0)
    codes = (blocks / scale).astype(np.float32).astype(dtype).astype(np.float64)
    return np.moveaxis((codes * scale).reshape(v.shape), -1, axis)


WIDE = False


def mx_kscale(k):
    if not WIDE:
        return np.ones(k)
    levels = np.array([10, -10, 5, -5, 0])
    if k % 512:
        return np.exp2(np.random.permutation(np.resize(levels, k // 32))).repeat(32)
    a = np.empty((k // 512, 16))
    for p in range(k // 512):
        a[p, :8] = np.random.permutation(np.resize(levels, 8))
        for g in range(8):
            far = levels[np.abs(levels - a[p, g]) >= 10]
            a[p, g + 8] = far[np.random.randint(len(far))]
    return np.exp2(a.ravel()).repeat(32)


def f64(x):
    return np.asarray(x).astype(np.float64)


def striped(idx):
    return np.tile(np.asarray(idx).reshape(-1, 16).T, (8, 1)).astype(np.uint16)


def unstriped(offs):
    return offs[:16].T.reshape(-1).astype(np.int64)


E2M1 = np.array([0.0, 0.5, 1.0, 1.5, 2.0, 3.0, 4.0, 6.0, -0.0, -0.5, -1.0, -1.5, -2.0, -3.0, -4.0, -6.0])


def pack_weight(w, fmt):
    k, n = w.shape
    w = f64(np.asarray(w, np.float32).astype(ml_dtypes.bfloat16)).reshape(k // 32, 32, n)
    amax = np.abs(w).max(1)
    if fmt == "e4m3":
        byte = np.frexp(amax)[1] - 1 + 127 - 7
    else:
        mant, ex = np.frexp(amax / 6.0)
        byte = np.where(mant > 0.5, ex, ex - 1) + 127
    byte = np.clip(np.where(amax > 0, byte, 1), 1, 254)
    scaled = (w * np.exp2(127.0 - byte)[:, None, :]).reshape(k, n).astype(np.float32)
    by_word = np.ascontiguousarray(scaled.reshape(k // 512, 128, 4, n).transpose(0, 1, 3, 2))
    if fmt == "e4m3":
        words = by_word.astype(ml_dtypes.float8_e4m3fn).view(np.uint8)
    else:
        c = by_word.astype(ml_dtypes.float4_e2m1fn).view(np.uint8) & 0xF
        words = (c[..., 0::2] | (c[..., 1::2] << 4)).reshape(k // 512, 128, 2 * n)
    return np.ascontiguousarray(words), np.ascontiguousarray(byte.astype(np.uint8).reshape(k // 512, 16, n))


def unpack_weight(words, scales, fmt):
    g, _, n = scales.shape
    words = np.ascontiguousarray(words).reshape(g, 128, n, -1)
    if fmt == "e4m3":
        vals = words.view(ml_dtypes.float8_e4m3fn).astype(np.float64)
    else:
        nib = np.empty((g, 128, n, 4), np.uint8)
        nib[..., 0::2] = words & 0xF
        nib[..., 1::2] = words >> 4
        vals = E2M1[nib]
    vals = vals * np.repeat(np.exp2(scales.astype(np.float64) - 127.0), 8, axis=1)[..., None]
    return vals.transpose(0, 1, 3, 2).reshape(g * 512, n)


K, T, J, R, N = 1024, 1024, 512, 512, 512


def setup_inputs():
    n = np.random.standard_normal
    idx = np.random.permutation(T)[:J]
    fk = mx_kscale(K)
    fr = mx_kscale(R)
    xtp = pack_weight(n((K, T)) * np.random.uniform(0.3, 1.9, (1, T)) / fk[:, None], "e4m3")
    wap = pack_weight(n((K, R)) * 1 / np.sqrt(K) * fk[:, None], "e2m1")
    wbp = pack_weight(n((R, N)) * 1 / np.sqrt(R) / fr[:, None], "e4m3")
    return {
        "xt_words": xtp[0],
        "xt_scales": xtp[1],
        "wa_words": wap[0],
        "wa_scales": wap[1],
        "fr": (np.random.uniform(0.5, 2.0, (R, 1)) * fr[:, None]).astype(np.float32),
        "wb_words": wbp[0],
        "wb_scales": wbp[1],
        "rw": (np.random.uniform(0.5, 2.0, (1, J))).astype(np.float32),
        "offs": striped(idx),
    }


def reference(xt_words, xt_scales, wa_words, wa_scales, fr, wb_words, wb_scales, rw, offs):
    idx = unstriped(offs)
    xtu = unpack_weight(xt_words, xt_scales, "e4m3")
    wau = unpack_weight(wa_words, wa_scales, "e2m1")
    wbu = unpack_weight(wb_words, wb_scales, "e4m3")
    xtidxg = xtu[:, idx]
    z = xtidxg.T @ wau
    e = np.mean(np.square(z), axis=1, keepdims=True)
    h1 = z * e / (e + 1.0)
    ht = h1.T
    hid = ht * f64(fr)
    hidq = mxq(hid, 0, "e4m3")
    p = wbu.T @ hidq
    y = p * f64(rw)
    return y

@@ -1,0 +1,167 @@
+from contextlib import ExitStack
+
+import concourse.mybir as mybir
+from concourse.masks import make_identity
+
+K, T, J, R, N = 1024, 1024, 512, 512, 512
+FLOPS = 2 * K * J * R + 2 * R * N * J
+
+F32 = mybir.dt.float32
+BF16 = mybir.dt.bfloat16
+I32 = mybir.dt.int32
+U32 = mybir.dt.uint32
+U16 = mybir.dt.uint16
+U8 = mybir.dt.uint8
+FP8X4 = mybir.dt.float8_e4m3fn_x4
+FP4X4 = mybir.dt.float4_e2m1fn_x4
+ALU = mybir.AluOpType
+ACT = mybir.ActivationFunctionType
+
+P = 128
+PASSES = K // 512
+TILES = J // P
+
+
+def load_scales(queue, plane, scales):
+    passes = scales.shape[0]
+    rows = scales.bitcast(I32)
+    for r in range(4):
+        queue.dma_start(
+            out=plane[r:P:32, :].bitcast(I32).rearrange("p (z c) -> p z c", z=passes),
+            in_=rows[:, r:16:4, :].rearrange("z q c -> q z c"),
+        )
+
+
+def tile_moe_expert_hidden_by_energy_kernel(
+    tc, xt_words, xt_scales, wa_words, wa_scales, fr, wb_words, wb_scales, rw, offs, out
+):
+    nc = tc.nc
+    with ExitStack() as ctx:
+        keep = ctx.enter_context(tc.tile_pool(name="keep", bufs=1))
+        work = ctx.enter_context(tc.tile_pool(name="work", bufs=TILES))
+        zpool = ctx.enter_context(tc.psum_pool(name="zpool", bufs=TILES))
+        tpool = ctx.enter_context(tc.psum_pool(name="tpool", bufs=TILES))
+
+        offsets = keep.tile([P, J // 16], U16, name="offsets")
+        xw = [keep.tile([P, T], I32, name="xw%d" % z, align_bytes=64) for z in range(PASSES)]
+        xs = keep.tile([P, PASSES * T], U8, name="xs", align_bytes=64)
+        waw = keep.tile([P, PASSES, 2 * R], U8, name="waw", align_bytes=64)
+        was = keep.tile([P, PASSES * R], U8, name="was", align_bytes=64)
+        wbw = keep.tile([P, N], I32, name="wbw", align_bytes=64)
+        wbs = keep.tile([P, N], U8, name="wbs", align_bytes=64)
+        fr4 = keep.tile([P, 4], F32, name="fr4")
+        rw4 = keep.tile([P, 4], F32, name="rw4")
+        ident = keep.tile([P, P], F32, name="ident")
+        frb = keep.tile([P, R], F32, name="frb", tag="frb_then_res")
+        rwb = keep.tile([P, J], F32, name="rwb")
+        gw = [keep.tile([P, J], U32, name="gw%d" % z, align_bytes=64) for z in range(PASSES)]
+        gs = [keep.tile([P, J], U8, name="gs%d" % z, align_bytes=64) for z in range(PASSES)]
+
+        nc.vector.memset(xs[:].bitcast(I32), 0)
+        nc.vector.memset(was[:].bitcast(I32), 0)
+        nc.vector.memset(wbs[:].bitcast(I32), 0)
+
+        def load_words(tile, words):
+            nc.sync.dma_start(out=tile[:], in_=words.rearrange("p n t -> p (n t)").bitcast(I32))
+
+        make_identity(nc, ident[:])
+        nc.sync.dma_start(offsets[:], offs)
+        load_words(xw[0], xt_words[0])
+        load_scales(nc.sync, xs, xt_scales)
+        nc.sync.dma_start(out=waw[:].bitcast(I32), in_=wa_words.bitcast(I32).rearrange("z p c -> p z c"))
+        load_words(xw[1], xt_words[1])
+        load_scales(nc.sync, was, wa_scales)
+        load_words(wbw, wb_words[0])
+        load_scales(nc.sync, wbs, wb_scales)
+        nc.gpsimd.dma_start(out=fr4[:], in_=fr.rearrange("(p c) o -> p (c o)", c=4))
+        nc.gpsimd.dma_start(out=rw4[:], in_=rw.rearrange("o (p c) -> p (o c)", c=4))
+
+        for small, wide in ((fr4, frb), (rw4, rwb)):
+            spread = tpool.tile([P, 4, P], F32, name="tbank")
+            for m in range(4):
+                nc.tensor.transpose(spread[:, m, :], small[:, m : m + 1].to_broadcast([P, P]), ident[:])
+            nc.scalar.activation(
+                out=wide[:].rearrange("p (n m) -> p n m", m=4),
+                in_=spread[:].rearrange("p m n -> p n m"),
+                func=ACT.Copy,
+            )
+
+        zb = [zpool.tile([P, R], F32, name="zbank") for jt in range(TILES)]
+
+        def first_layer(z, jt):
+            cols = slice(jt * P, (jt + 1) * P)
+            nc.tensor.matmul_mx(
+                out=zb[jt][:],
+                lhsT=gw[z][:, cols].bitcast(FP8X4),
+                lhsT_scale=gs[z][:, cols],
+                rhs=waw[:, z, :].bitcast(FP4X4),
+                rhs_scale=was[:, z * R : (z + 1) * R],
+                start=(z == 0),
+                stop=(z == PASSES - 1),
+            )
+
+        nc.vector.tensor_copy(gw[0][:], xw[0][:].bitcast(U32).indirect(offsets[:]))
+        for z in range(PASSES):
+            nc.vector.tensor_copy(gs[z][:], xs[:, z * T : (z + 1) * T].indirect(offsets[:]))
+        for jt in range(TILES):
+            listed = offsets[:, jt * P // 16 : (jt + 1) * P // 16]
+            nc.vector.tensor_copy(gw[1][:, jt * P : (jt + 1) * P], xw[1][:].bitcast(U32).indirect(listed))
+        for jt in range(TILES - 1):
+            first_layer(0, jt)
+        first_layer(1, 0)
+        first_layer(0, TILES - 1)
+        for jt in range(1, TILES):
+            first_layer(1, jt)
+
+        rows = []
+        for jt in range(TILES):
+            squares = work.tile([P, R], F32, name="squares")
+            total = work.tile([P, 1], F32, name="total")
+            nc.scalar.activation(out=squares[:], in_=zb[jt][:], func=ACT.Square, accum_out=total[:])
+            den = work.tile([P, 1], F32, name="den")
+            nc.gpsimd.tensor_scalar(den[:], total[:], 1.0, float(R), ALU.mult, ALU.add)
+            rec = work.tile([P, 1], F32, name="rec")
+            nc.vector.reciprocal(rec[:], den[:])
+            gain = work.tile([P, 1], F32, name="gain")
+            nc.vector.tensor_tensor(gain[:], total[:], rec[:], ALU.mult)
+            row = work.tile([P, R], BF16, name="row", align_bytes=64)
+            nc.vector.scalar_tensor_tensor(row[:], zb[jt][:], gain[:], frb[:], ALU.mult, ALU.mult)
+            rows.append(row)
+
+        codes = []
+        for jt in range(TILES):
+            pairs = rows[jt][:].bitcast(F32)
+            turned = tpool.tile([P, 2, P], F32, name="tbank")
+            for u in range(2):
+                nc.tensor.transpose(turned[:, u, :], pairs[:, u : R // 2 : 2], ident[:])
+            hid = work.tile([P, 4 * P], BF16, name="hid", align_bytes=64)
+            nc.scalar.copy(
+                out=hid[:].bitcast(F32).rearrange("p (j u) -> p j u", u=2),
+                in_=turned[:].rearrange("p u j -> p j u"),
+            )
+            hw = work.tile([P, P], U32, name="hw", align_bytes=64)
+            hs = work.tile([P, P], U8, name="hs", align_bytes=64)
+            nc.vector.quantize_mx(out=hw[:].bitcast(FP8X4), scales=hs[:], in_=hid[:])
+            codes.append((hw, hs))
+
+        out_v = out.rearrange("(t p) j -> p t j", p=P)
+        res = keep.tile([P, TILES, 4, P], F32, name="res", tag="frb_then_res")
+        for jt in range(TILES):
+            cols = slice(jt * P, (jt + 1) * P)
+            hw, hs = codes[jt]
+            prod = zpool.tile([P, 4, P], F32, name="zbank")
+            for t in range(4):
+                ncols = slice(t * P, (t + 1) * P)
+                nc.tensor.matmul_mx(
+                    out=prod[:, t, :],
+                    lhsT=wbw[:, ncols].bitcast(FP8X4),
+                    lhsT_scale=wbs[:, ncols],
+                    rhs=hw[:].bitcast(FP8X4),
+                    rhs_scale=hs[:],
+                    start=True,
+                    stop=True,
+                )
+            nc.vector.tensor_tensor(
+                res[:, jt], prod[:], rwb[:, cols].unsqueeze(1).to_broadcast([P, 4, P]), ALU.mult
+            )
+            nc.sync.dma_start(out=out_v[:, :, cols], in_=res[:, jt])

@@ -20,6 +20,8 @@ ACT = mybir.ActivationFunctionType
 P = 128
 PASSES = K // 512
 TILES = J // P
+WARM = 3
+GROUPS = ((0,), (1,), (2, 3))
 
 
 def load_scales(queue, plane, scales):
@@ -39,6 +41,7 @@ def tile_moe_expert_hidden_by_energy_kernel(
     with ExitStack() as ctx:
         keep = ctx.enter_context(tc.tile_pool(name="keep", bufs=1))
         work = ctx.enter_context(tc.tile_pool(name="work", bufs=TILES))
+        ring = ctx.enter_context(tc.tile_pool(name="ring", bufs=2))
         zpool = ctx.enter_context(tc.psum_pool(name="zpool", bufs=TILES))
         tpool = ctx.enter_context(tc.psum_pool(name="tpool", bufs=TILES))
 
@@ -54,7 +57,6 @@ def tile_moe_expert_hidden_by_energy_kernel(
         ident = keep.tile([P, P], F32, name="ident")
         frb = keep.tile([P, R], F32, name="frb", tag="frb_then_res")
         rwb = keep.tile([P, J], F32, name="rwb")
-        gw = [keep.tile([P, J], U32, name="gw%d" % z, align_bytes=64) for z in range(PASSES)]
         gs = [keep.tile([P, J], U8, name="gs%d" % z, align_bytes=64) for z in range(PASSES)]
 
         nc.vector.memset(xs[:].bitcast(I32), 0)
@@ -66,15 +68,15 @@ def tile_moe_expert_hidden_by_energy_kernel(
 
         make_identity(nc, ident[:])
         nc.sync.dma_start(offsets[:], offs)
-        load_words(xw[0], xt_words[0])
+        nc.sync.dma_start(out=fr4[:], in_=fr.rearrange("(p c) o -> p (c o)", c=4))
+        nc.sync.dma_start(out=rw4[:], in_=rw.rearrange("o (p c) -> p (o c)", c=4))
         load_scales(nc.sync, xs, xt_scales)
+        for z in range(PASSES):
+            load_words(xw[z], xt_words[z])
         nc.sync.dma_start(out=waw[:].bitcast(I32), in_=wa_words.bitcast(I32).rearrange("z p c -> p z c"))
-        load_words(xw[1], xt_words[1])
         load_scales(nc.sync, was, wa_scales)
         load_words(wbw, wb_words[0])
         load_scales(nc.sync, wbs, wb_scales)
-        nc.gpsimd.dma_start(out=fr4[:], in_=fr.rearrange("(p c) o -> p (c o)", c=4))
-        nc.gpsimd.dma_start(out=rw4[:], in_=rw.rearrange("o (p c) -> p (o c)", c=4))
 
         for small, wide in ((fr4, frb), (rw4, rwb)):
             spread = tpool.tile([P, 4, P], F32, name="tbank")
@@ -88,45 +90,53 @@ def tile_moe_expert_hidden_by_energy_kernel(
 
         zb = [zpool.tile([P, R], F32, name="zbank") for jt in range(TILES)]
 
-        def first_layer(z, jt):
-            cols = slice(jt * P, (jt + 1) * P)
-            nc.tensor.matmul_mx(
-                out=zb[jt][:],
-                lhsT=gw[z][:, cols].bitcast(FP8X4),
-                lhsT_scale=gs[z][:, cols],
-                rhs=waw[:, z, :].bitcast(FP4X4),
-                rhs_scale=was[:, z * R : (z + 1) * R],
-                start=(z == 0),
-                stop=(z == PASSES - 1),
-            )
-
-        nc.vector.tensor_copy(gw[0][:], xw[0][:].bitcast(U32).indirect(offsets[:]))
         for z in range(PASSES):
             nc.vector.tensor_copy(gs[z][:], xs[:, z * T : (z + 1) * T].indirect(offsets[:]))
+
+        warm = tpool.tile([P, R], F32, name="tbank")
+        for w in range(WARM):
+            nc.tensor.matmul_mx(
+                out=warm[:],
+                lhsT=xw[0][:, 0:P].bitcast(FP8X4),
+                lhsT_scale=xs[:, 0:P],
+                rhs=xw[0][:, 0:R].bitcast(FP8X4),
+                rhs_scale=xs[:, 0:R],
+                start=True,
+                stop=True,
+            )
+
         for jt in range(TILES):
+            cols = slice(jt * P, (jt + 1) * P)
             listed = offsets[:, jt * P // 16 : (jt + 1) * P // 16]
-            nc.vector.tensor_copy(gw[1][:, jt * P : (jt + 1) * P], xw[1][:].bitcast(U32).indirect(listed))
-        for jt in range(TILES - 1):
-            first_layer(0, jt)
-        first_layer(1, 0)
-        first_layer(0, TILES - 1)
-        for jt in range(1, TILES):
-            first_layer(1, jt)
+            for z in range(PASSES):
+                gw = ring.tile([P, P], U32, name="gw%d" % z, align_bytes=64)
+                nc.vector.tensor_copy(gw[:], xw[z][:].bitcast(U32).indirect(listed))
+                nc.tensor.matmul_mx(
+                    out=zb[jt][:],
+                    lhsT=gw[:].bitcast(FP8X4),
+                    lhsT_scale=gs[z][:, cols],
+                    rhs=waw[:, z, :].bitcast(FP4X4),
+                    rhs_scale=was[:, z * R : (z + 1) * R],
+                    start=(z == 0),
+                    stop=(z == PASSES - 1),
+                )
 
         rows = []
-        for jt in range(TILES):
-            squares = work.tile([P, R], F32, name="squares")
-            total = work.tile([P, 1], F32, name="total")
-            nc.scalar.activation(out=squares[:], in_=zb[jt][:], func=ACT.Square, accum_out=total[:])
-            den = work.tile([P, 1], F32, name="den")
+        for group in GROUPS:
+            total = work.tile([P, len(group)], F32, name="total")
+            for i, jt in enumerate(group):
+                squares = work.tile([P, R], F32, name="squares")
+                nc.scalar.activation(out=squares[:], in_=zb[jt][:], func=ACT.Square, accum_out=total[:, i : i + 1])
+            den = work.tile([P, len(group)], F32, name="den")
             nc.gpsimd.tensor_scalar(den[:], total[:], 1.0, float(R), ALU.mult, ALU.add)
-            rec = work.tile([P, 1], F32, name="rec")
+            rec = work.tile([P, len(group)], F32, name="rec")
             nc.vector.reciprocal(rec[:], den[:])
-            gain = work.tile([P, 1], F32, name="gain")
+            gain = work.tile([P, len(group)], F32, name="gain")
             nc.vector.tensor_tensor(gain[:], total[:], rec[:], ALU.mult)
-            row = work.tile([P, R], BF16, name="row", align_bytes=64)
-            nc.vector.scalar_tensor_tensor(row[:], zb[jt][:], gain[:], frb[:], ALU.mult, ALU.mult)
-            rows.append(row)
+            for i, jt in enumerate(group):
+                row = work.tile([P, R], BF16, name="row", align_bytes=64)
+                nc.vector.scalar_tensor_tensor(row[:], zb[jt][:], gain[:, i : i + 1], frb[:], ALU.mult, ALU.mult)
+                rows.append(row)
 
         codes = []
         for jt in range(TILES):
@@ -149,19 +159,22 @@ def tile_moe_expert_hidden_by_energy_kernel(
         for jt in range(TILES):
             cols = slice(jt * P, (jt + 1) * P)
             hw, hs = codes[jt]
-            prod = zpool.tile([P, 4, P], F32, name="zbank")
-            for t in range(4):
-                ncols = slice(t * P, (t + 1) * P)
-                nc.tensor.matmul_mx(
-                    out=prod[:, t, :],
-                    lhsT=wbw[:, ncols].bitcast(FP8X4),
-                    lhsT_scale=wbs[:, ncols],
-                    rhs=hw[:].bitcast(FP8X4),
-                    rhs_scale=hs[:],
-                    start=True,
-                    stop=True,
+            share = 2 if jt == TILES - 1 else 4
+            for first in range(0, 4, share):
+                prod = zpool.tile([P, share, P], F32, name="zbank")
+                for t in range(share):
+                    ncols = slice((first + t) * P, (first + t + 1) * P)
+                    nc.tensor.matmul_mx(
+                        out=prod[:, t, :],
+                        lhsT=wbw[:, ncols].bitcast(FP8X4),
+                        lhsT_scale=wbs[:, ncols],
+                        rhs=hw[:].bitcast(FP8X4),
+                        rhs_scale=hs[:],
+                        start=True,
+                        stop=True,
+                    )
+                part = res[:, jt, first : first + share, :]
+                nc.vector.tensor_tensor(
+                    part, prod[:], rwb[:, cols].unsqueeze(1).to_broadcast([P, share, P]), ALU.mult
                 )
-            nc.vector.tensor_tensor(
-                res[:, jt], prod[:], rwb[:, cols].unsqueeze(1).to_broadcast([P, 4, P]), ALU.mult
-            )
-            nc.sync.dma_start(out=out_v[:, :, cols], in_=res[:, jt])
+                nc.sync.dma_start(out=out_v[:, first : first + share, cols], in_=part)

@@ -135,7 +135,18 @@ def tile_moe_expert_hidden_by_energy_kernel(
             nc.vector.tensor_tensor(gain[:], total[:], rec[:], ALU.mult)
             for i, jt in enumerate(group):
                 row = work.tile([P, R], BF16, name="row", align_bytes=64)
-                nc.vector.scalar_tensor_tensor(row[:], zb[jt][:], gain[:, i : i + 1], frb[:], ALU.mult, ALU.mult)
+                if jt < TILES - 1:
+                    nc.vector.scalar_tensor_tensor(row[:], zb[jt][:], gain[:, i : i + 1], frb[:], ALU.mult, ALU.mult)
+                else:
+                    for u in range(2):
+                        nc.vector.scalar_tensor_tensor(
+                            row[:, u * R // 2 : (u + 1) * R // 2].rearrange("p (m e) -> p m e", e=2),
+                            zb[jt][:].rearrange("p (m u e) -> p u m e", u=2, e=2)[:, u],
+                            gain[:, i : i + 1],
+                            frb[:].rearrange("p (m u e) -> p u m e", u=2, e=2)[:, u],
+                            ALU.mult,
+                            ALU.mult,
+                        )
                 rows.append(row)
 
         codes = []
@@ -143,7 +154,8 @@ def tile_moe_expert_hidden_by_energy_kernel(
             pairs = rows[jt][:].bitcast(F32)
             turned = tpool.tile([P, 2, P], F32, name="tbank")
             for u in range(2):
-                nc.tensor.transpose(turned[:, u, :], pairs[:, u : R // 2 : 2], ident[:])
+                picked = pairs[:, u : R // 2 : 2] if jt < TILES - 1 else pairs[:, u * P : (u + 1) * P]
+                nc.tensor.transpose(turned[:, u, :], picked, ident[:])
             hid = work.tile([P, 4 * P], BF16, name="hid", align_bytes=64)
             nc.scalar.copy(
                 out=hid[:].bitcast(F32).rearrange("p (j u) -> p j u", u=2),

from contextlib import ExitStack

import concourse.mybir as mybir
from concourse.masks import make_identity

K, T, J, R, N = 1024, 1024, 512, 512, 512
FLOPS = 2 * K * J * R + 2 * R * N * J

F32 = mybir.dt.float32
BF16 = mybir.dt.bfloat16
I32 = mybir.dt.int32
U32 = mybir.dt.uint32
U16 = mybir.dt.uint16
U8 = mybir.dt.uint8
FP8X4 = mybir.dt.float8_e4m3fn_x4
FP4X4 = mybir.dt.float4_e2m1fn_x4
ALU = mybir.AluOpType
ACT = mybir.ActivationFunctionType

P = 128
PASSES = K // 512
TILES = J // P
WARM = 3
GROUPS = ((0,), (1,), (2, 3))


def load_scales(queue, plane, scales):
    passes = scales.shape[0]
    rows = scales.bitcast(I32)
    for r in range(4):
        queue.dma_start(
            out=plane[r:P:32, :].bitcast(I32).rearrange("p (z c) -> p z c", z=passes),
            in_=rows[:, r:16:4, :].rearrange("z q c -> q z c"),
        )


def tile_moe_expert_hidden_by_energy_kernel(
    tc, xt_words, xt_scales, wa_words, wa_scales, fr, wb_words, wb_scales, rw, offs, out
):
    nc = tc.nc
    with ExitStack() as ctx:
        keep = ctx.enter_context(tc.tile_pool(name="keep", bufs=1))
        work = ctx.enter_context(tc.tile_pool(name="work", bufs=TILES))
        ring = ctx.enter_context(tc.tile_pool(name="ring", bufs=2))
        zpool = ctx.enter_context(tc.psum_pool(name="zpool", bufs=TILES))
        tpool = ctx.enter_context(tc.psum_pool(name="tpool", bufs=TILES))

        offsets = keep.tile([P, J // 16], U16, name="offsets")
        xw = [keep.tile([P, T], I32, name="xw%d" % z, align_bytes=64) for z in range(PASSES)]
        xs = keep.tile([P, PASSES * T], U8, name="xs", align_bytes=64)
        waw = keep.tile([P, PASSES, 2 * R], U8, name="waw", align_bytes=64)
        was = keep.tile([P, PASSES * R], U8, name="was", align_bytes=64)
        wbw = keep.tile([P, N], I32, name="wbw", align_bytes=64)
        wbs = keep.tile([P, N], U8, name="wbs", align_bytes=64)
        fr4 = keep.tile([P, 4], F32, name="fr4")
        rw4 = keep.tile([P, 4], F32, name="rw4")
        ident = keep.tile([P, P], F32, name="ident")
        frb = keep.tile([P, R], F32, name="frb", tag="frb_then_res")
        rwb = keep.tile([P, J], F32, name="rwb")
        gs = [keep.tile([P, J], U8, name="gs%d" % z, align_bytes=64) for z in range(PASSES)]

        nc.vector.memset(xs[:].bitcast(I32), 0)
        nc.vector.memset(was[:].bitcast(I32), 0)
        nc.vector.memset(wbs[:].bitcast(I32), 0)

        def load_words(tile, words):
            nc.sync.dma_start(out=tile[:], in_=words.rearrange("p n t -> p (n t)").bitcast(I32))

        make_identity(nc, ident[:])
        nc.sync.dma_start(offsets[:], offs)
        nc.sync.dma_start(out=fr4[:], in_=fr.rearrange("(p c) o -> p (c o)", c=4))
        nc.sync.dma_start(out=rw4[:], in_=rw.rearrange("o (p c) -> p (o c)", c=4))
        load_scales(nc.sync, xs, xt_scales)
        for z in range(PASSES):
            load_words(xw[z], xt_words[z])
        nc.sync.dma_start(out=waw[:].bitcast(I32), in_=wa_words.bitcast(I32).rearrange("z p c -> p z c"))
        load_scales(nc.sync, was, wa_scales)
        load_words(wbw, wb_words[0])
        load_scales(nc.sync, wbs, wb_scales)

        for small, wide in ((fr4, frb), (rw4, rwb)):
            spread = tpool.tile([P, 4, P], F32, name="tbank")
            for m in range(4):
                nc.tensor.transpose(spread[:, m, :], small[:, m : m + 1].to_broadcast([P, P]), ident[:])
            nc.scalar.activation(
                out=wide[:].rearrange("p (n m) -> p n m", m=4),
                in_=spread[:].rearrange("p m n -> p n m"),
                func=ACT.Copy,
            )

        zb = [zpool.tile([P, R], F32, name="zbank") for jt in range(TILES)]

        for z in range(PASSES):
            nc.vector.tensor_copy(gs[z][:], xs[:, z * T : (z + 1) * T].indirect(offsets[:]))

        warm = tpool.tile([P, R], F32, name="tbank")
        for w in range(WARM):
            nc.tensor.matmul_mx(
                out=warm[:],
                lhsT=xw[0][:, 0:P].bitcast(FP8X4),
                lhsT_scale=xs[:, 0:P],
                rhs=xw[0][:, 0:R].bitcast(FP8X4),
                rhs_scale=xs[:, 0:R],
                start=True,
                stop=True,
            )

        for jt in range(TILES):
            cols = slice(jt * P, (jt + 1) * P)
            listed = offsets[:, jt * P // 16 : (jt + 1) * P // 16]
            for z in range(PASSES):
                gw = ring.tile([P, P], U32, name="gw%d" % z, align_bytes=64)
                nc.vector.tensor_copy(gw[:], xw[z][:].bitcast(U32).indirect(listed))
                nc.tensor.matmul_mx(
                    out=zb[jt][:],
                    lhsT=gw[:].bitcast(FP8X4),
                    lhsT_scale=gs[z][:, cols],
                    rhs=waw[:, z, :].bitcast(FP4X4),
                    rhs_scale=was[:, z * R : (z + 1) * R],
                    start=(z == 0),
                    stop=(z == PASSES - 1),
                )

        rows = []
        for group in GROUPS:
            total = work.tile([P, len(group)], F32, name="total")
            for i, jt in enumerate(group):
                squares = work.tile([P, R], F32, name="squares")
                nc.scalar.activation(out=squares[:], in_=zb[jt][:], func=ACT.Square, accum_out=total[:, i : i + 1])
            den = work.tile([P, len(group)], F32, name="den")
            nc.gpsimd.tensor_scalar(den[:], total[:], 1.0, float(R), ALU.mult, ALU.add)
            rec = work.tile([P, len(group)], F32, name="rec")
            nc.vector.reciprocal(rec[:], den[:])
            gain = work.tile([P, len(group)], F32, name="gain")
            nc.vector.tensor_tensor(gain[:], total[:], rec[:], ALU.mult)
            for i, jt in enumerate(group):
                row = work.tile([P, R], BF16, name="row", align_bytes=64)
                if jt < TILES - 1:
                    nc.vector.scalar_tensor_tensor(row[:], zb[jt][:], gain[:, i : i + 1], frb[:], ALU.mult, ALU.mult)
                else:
                    for u in range(2):
                        nc.vector.scalar_tensor_tensor(
                            row[:, u * R // 2 : (u + 1) * R // 2].rearrange("p (m e) -> p m e", e=2),
                            zb[jt][:].rearrange("p (m u e) -> p u m e", u=2, e=2)[:, u],
                            gain[:, i : i + 1],
                            frb[:].rearrange("p (m u e) -> p u m e", u=2, e=2)[:, u],
                            ALU.mult,
                            ALU.mult,
                        )
                rows.append(row)

        codes = []
        for jt in range(TILES):
            pairs = rows[jt][:].bitcast(F32)
            turned = tpool.tile([P, 2, P], F32, name="tbank")
            for u in range(2):
                picked = pairs[:, u : R // 2 : 2] if jt < TILES - 1 else pairs[:, u * P : (u + 1) * P]
                nc.tensor.transpose(turned[:, u, :], picked, ident[:])
            hid = work.tile([P, 4 * P], BF16, name="hid", align_bytes=64)
            nc.scalar.copy(
                out=hid[:].bitcast(F32).rearrange("p (j u) -> p j u", u=2),
                in_=turned[:].rearrange("p u j -> p j u"),
            )
            hw = work.tile([P, P], U32, name="hw", align_bytes=64)
            hs = work.tile([P, P], U8, name="hs", align_bytes=64)
            nc.vector.quantize_mx(out=hw[:].bitcast(FP8X4), scales=hs[:], in_=hid[:])
            codes.append((hw, hs))

        out_v = out.rearrange("(t p) j -> p t j", p=P)
        res = keep.tile([P, TILES, 4, P], F32, name="res", tag="frb_then_res")
        for jt in range(TILES):
            cols = slice(jt * P, (jt + 1) * P)
            hw, hs = codes[jt]
            share = 2 if jt == TILES - 1 else 4
            for first in range(0, 4, share):
                prod = zpool.tile([P, share, P], F32, name="zbank")
                for t in range(share):
                    ncols = slice((first + t) * P, (first + t + 1) * P)
                    nc.tensor.matmul_mx(
                        out=prod[:, t, :],
                        lhsT=wbw[:, ncols].bitcast(FP8X4),
                        lhsT_scale=wbs[:, ncols],
                        rhs=hw[:].bitcast(FP8X4),
                        rhs_scale=hs[:],
                        start=True,
                        stop=True,
                    )
                part = res[:, jt, first : first + share, :]
                nc.vector.tensor_tensor(
                    part, prod[:], rwb[:, cols].unsqueeze(1).to_broadcast([P, share, P]), ALU.mult
                )
                nc.sync.dma_start(out=out_v[:, first : first + share, cols], in_=part)
